import numpy as np
import ml_dtypes


def mxq(x, axis, fmt="e4m3"):
    dtype, down = {"e4m3": (ml_dtypes.float8_e4m3fn, 7), "e5m2": (ml_dtypes.float8_e5m2, 14)}[fmt]
    v = np.moveaxis(np.asarray(x, np.float32).astype(ml_dtypes.bfloat16).astype(np.float64), axis, -1)
    blocks = v.reshape(v.shape[:-1] + (-1, 32))
    amax = np.abs(blocks).max(-1, keepdims=True)
    byte = np.maximum(np.where(amax > 0, np.frexp(amax)[1] - 1 + 127, 0) - down, 1)
    scale = np.exp2(byte - 127.0)
    codes = (blocks / scale).astype(np.float32).astype(dtype).astype(np.float64)
    return np.moveaxis((codes * scale).reshape(v.shape), -1, axis)


WIDE = False


def mx_kscale(k):
    if not WIDE:
        return np.ones(k)
    levels = np.array([10, -10, 5, -5, 0])
    if k % 512:
        return np.exp2(np.random.permutation(np.resize(levels, k // 32))).repeat(32)
    a = np.empty((k // 512, 16))
    for p in range(k // 512):
        a[p, :8] = np.random.permutation(np.resize(levels, 8))
        for g in range(8):
            far = levels[np.abs(levels - a[p, g]) >= 10]
            a[p, g + 8] = far[np.random.randint(len(far))]
    return np.exp2(a.ravel()).repeat(32)


def f64(x):
    return np.asarray(x).astype(np.float64)


def striped(idx):
    return np.tile(idx.reshape(-1, 16).T, (8, 1)).astype(np.uint16)


def unstriped(offs):
    return offs[:16].T.reshape(-1).astype(np.int64)


E2M1 = np.array([0.0, 0.5, 1.0, 1.5, 2.0, 3.0, 4.0, 6.0, -0.0, -0.5, -1.0, -1.5, -2.0, -3.0, -4.0, -6.0])


def pack_weight(w, fmt):
    k, n = w.shape
    w = f64(np.asarray(w, np.float32).astype(ml_dtypes.bfloat16)).reshape(k // 32, 32, n)
    amax = np.abs(w).max(1)
    if fmt == "e4m3":
        byte = np.frexp(amax)[1] - 1 + 127 - 7
    else:
        mant, ex = np.frexp(amax / 6.0)
        byte = np.where(mant > 0.5, ex, ex - 1) + 127
    byte = np.clip(np.where(amax > 0, byte, 1), 1, 254)
    scaled = (w * np.exp2(127.0 - byte)[:, None, :]).reshape(k, n).astype(np.float32)
    by_word = np.ascontiguousarray(scaled.reshape(k // 512, 128, 4, n).transpose(0, 1, 3, 2))
    if fmt == "e4m3":
        words = by_word.astype(ml_dtypes.float8_e4m3fn).view(np.uint8)
    else:
        c = by_word.astype(ml_dtypes.float4_e2m1fn).view(np.uint8) & 0xF
        words = (c[..., 0::2] | (c[..., 1::2] << 4)).reshape(k // 512, 128, 2 * n)
    return np.ascontiguousarray(words), np.ascontiguousarray(byte.astype(np.uint8).reshape(k // 512, 16, n))


def unpack_weight(words, scales, fmt):
    g, _, n = scales.shape
    words = np.ascontiguousarray(words).reshape(g, 128, n, -1)
    if fmt == "e4m3":
        vals = words.view(ml_dtypes.float8_e4m3fn).astype(np.float64)
    else:
        nib = np.empty((g, 128, n, 4), np.uint8)
        nib[..., 0::2] = words & 0xF
        nib[..., 1::2] = words >> 4
        vals = E2M1[nib]
    vals = vals * np.repeat(np.exp2(scales.astype(np.float64) - 127.0), 8, axis=1)[..., None]
    return vals.transpose(0, 1, 3, 2).reshape(g * 512, n)


def gelu(v):
    return 0.5 * v * (1.0 + np.tanh(np.sqrt(2.0 / np.pi) * (v + 0.044715 * v**3)))


K, H, N, T, S, P = 1024, 1024, 512, 2048, 1024, 512

def setup_inputs():
    n = np.random.standard_normal
    s = mx_kscale(K)[:, None]
    u = mx_kscale(H)[:, None]
    tab_words, tab_scales = pack_weight(n((K, T)) * s, "e4m3")
    w4_words, w4_scales = pack_weight(1.4 * n((H, N)) / np.sqrt(H) / u, "e2m1")
    return {
        "tab_words": tab_words, "tab_scales": tab_scales,
        "offs": striped(np.random.permutation(T)[:S]),
        "pos1": striped(np.random.permutation(S)[:P]),
        "pos2": striped(np.random.permutation(S)[:P]),
        "w1": (0.9 * n((K, H)) / np.sqrt(K) / s).astype(np.float32),
        "sharp": np.random.uniform(1, 3, H).astype(np.float32),
        "share": np.random.uniform(0.1, 0.5, H).astype(np.float32),
        "slope": np.random.uniform(0.6, 3.0, H).astype(np.float32),
        "thr": n(H).astype(np.float32),
        "score": (1.3 * n((H, P)) * u).astype(np.float32),
        "lean": (n(H) * u[:, 0]).astype(np.float32),
        "w4_words": w4_words, "w4_scales": w4_scales,
        "w2": (1.4 * n((H, N)) / np.sqrt(H) / u).astype(np.float32),
    }

def reference(tab_words, tab_scales, offs, pos1, pos2, w1, sharp, share, slope, thr, score, lean, w4_words, w4_scales, w2):
    v = unpack_weight(tab_words, tab_scales, "e4m3")[:, unstriped(offs)]
    h = mxq(f64(w1), 0, "e4m3").T @ v
    top = h.max(axis=1)
    a = 1.0 / (1.0 + np.exp(-f64(sharp)[:, None] * (h[:, unstriped(pos1)] - f64(share)[:, None] * top[:, None])))
    c = 1.0 / (1.0 + np.exp(-(f64(slope)[:, None] * h[:, unstriped(pos2)] + f64(thr)[:, None])))
    z = f64(score) * a + f64(lean)[:, None] * c
    zq = mxq(z, 0, "e4m3")
    d = unpack_weight(w4_words, w4_scales, "e2m1").T @ zq
    e = mxq(f64(w2), 0, "e4m3").T @ zq
    return d + np.abs(e)

@@ -1,0 +1,303 @@
+from contextlib import ExitStack
+
+import concourse.mybir as mybir
+
+K, H, N, T, S, PICK = 1024, 1024, 512, 2048, 1024, 512
+FLOPS = 2 * K * H * S + 2 * 2 * H * N * PICK
+
+F32 = mybir.dt.float32
+BF16 = mybir.dt.bfloat16
+I32 = mybir.dt.int32
+U32 = mybir.dt.uint32
+U16 = mybir.dt.uint16
+U8 = mybir.dt.uint8
+E4M3 = mybir.dt.float8_e4m3fn_x4
+E2M1 = mybir.dt.float4_e2m1fn_x4
+ALU = mybir.AluOpType
+ACT = mybir.ActivationFunctionType
+
+P = 128
+PACK = 4
+PASS = P * PACK
+BANK = 512
+HALF = 256
+PER_COL = 16
+
+
+def tile_list_band_adjudication_box_kernel(
+    tc, tab_words, tab_scales, offs, pos1, pos2, w1, sharp, share, slope, thr, score, lean, w4_words, w4_scales, w2, out
+):
+    nc = tc.nc
+
+    with ExitStack() as ctx:
+        keep = ctx.enter_context(tc.tile_pool(name="keep", bufs=1))
+        psum = ctx.enter_context(tc.psum_pool(name="psum", bufs=8))
+
+        def held(name, shape, dtype, tag=None):
+            return keep.tile(shape, dtype, name=name, tag=tag or name, align_bytes=64)
+
+        def cast(engine, dst, src):
+            if engine == "scalar":
+                nc.scalar.copy(out=dst, in_=src)
+            else:
+                nc.vector.tensor_copy(out=dst, in_=src)
+
+        tab_s = held("tab_s", [P, T], U8)
+        nc.vector.memset(tab_s[:].bitcast(I32), 0)
+        w4_s = held("w4_s", [P, 2, N], U8)
+        nc.gpsimd.memset(w4_s[:].rearrange("p b n -> p (b n)").bitcast(I32), 0)
+
+        idx = held("idx", [P, S // PER_COL], U16)
+        p1 = held("p1", [P, PICK // PER_COL], U16)
+        p2 = held("p2", [P, PICK // PER_COL], U16)
+        tab_w = [held("tab_w%d" % a, [P, T], I32) for a in range(2)]
+        w1_raw = {}
+        row = {}
+
+        def load_tab(a):
+            nc.sync.dma_start(out=tab_w[a][:], in_=tab_words[a].rearrange("p t i -> p (t i)").bitcast(I32))
+
+        def load_w1(a, c0, c1):
+            w1_raw[a, c0] = held("w1_raw%d_%d" % (a, c0), [P, PACK, c1 - c0], F32)
+            rows = w1[PASS * a : PASS * (a + 1), c0:c1]
+            nc.sync.dma_start(out=w1_raw[a, c0][:], in_=rows.rearrange("(p j) c -> p j c", j=PACK))
+
+        def load_rows(name, mat, b):
+            raw = held("%s%d" % (name, b), [P, PACK, mat.shape[1]], F32)
+            nc.sync.dma_start(out=raw[:], in_=mat[PASS * b : PASS * (b + 1), :].rearrange("(p i) c -> p i c", i=PACK))
+            return raw
+
+        def load_vector(name, vec):
+            row[name] = held(name, [P, 2 * PACK], F32)
+            nc.sync.dma_start(
+                out=row[name][:].rearrange("p (b i) -> p b i", i=PACK),
+                in_=vec.rearrange("(b p i) -> p b i", p=P, i=PACK),
+            )
+
+        nc.sync.dma_start(idx[:], offs)
+        load_tab(0)
+        for q in range(4):
+            nc.scalar.dma_start(
+                out=tab_s[32 * q : 32 * q + 8, :].bitcast(I32), in_=tab_scales[:, 4 * q : 4 * q + 4, :].bitcast(I32)
+            )
+        load_w1(0, 0, 512)
+        load_tab(1)
+        load_w1(1, 0, 256)
+        load_w1(1, 256, 512)
+        load_w1(0, 512, 768)
+        load_vector("slope", slope)
+        load_vector("thr", thr)
+        nc.sync.dma_start(p2[:], pos2)
+        load_w1(0, 768, 1024)
+        load_vector("sharp", sharp)
+        load_vector("share", share)
+        nc.sync.dma_start(p1[:], pos1)
+        load_w1(1, 512, 1024)
+        load_vector("lean", lean)
+        score_sb = [load_rows("score", score, 0)]
+        w2_raw = [load_rows("w2_raw", w2, 0), load_rows("w2_raw", w2, 1)]
+        score_sb.append(load_rows("score", score, 1))
+        w4_w = held("w4_w", [P, 2, 2 * N], U8)
+        nc.sync.dma_start(out=w4_w[:].bitcast(I32), in_=w4_words.rearrange("b p e -> p b e").bitcast(I32))
+        for q in range(4):
+            nc.sync.dma_start(
+                out=w4_s[32 * q : 32 * q + 4, :, :].bitcast(I32),
+                in_=w4_scales[:, 4 * q : 4 * q + 4, :].rearrange("b r n -> r b n").bitcast(I32),
+            )
+
+        v_w = [held("v_w%d" % a, [P, S], U32) for a in range(2)]
+        v_s = held("v_s", [P, S], U8)
+
+        def gather_words(a):
+            for s0 in range(0, S, BANK):
+                nc.vector.tensor_copy(
+                    out=v_w[a][:, s0 : s0 + BANK],
+                    in_=tab_w[a][:].bitcast(U32).indirect(idx[:, s0 // PER_COL : (s0 + BANK) // PER_COL]),
+                )
+
+        w1_bf = {(a, b): held("w1_bf%d%d" % (a, b), [P, PACK, P, PACK], BF16) for a in range(2) for b in range(2)}
+        w1_q = {(a, b): held("w1_q%d%d" % (a, b), [P, PASS], U32) for a in range(2) for b in range(2)}
+        w1_s = {(a, b): held("w1_s%d%d" % (a, b), [P, PASS], U8) for a in range(2) for b in range(2)}
+
+        def round_w1(engine, a, c0):
+            raw = w1_raw[a, c0]
+            b, m0 = c0 // PASS, (c0 % PASS) // PACK
+            m1 = m0 + raw.shape[2] // PACK
+            cast(
+                engine,
+                w1_bf[a, b][:, :, m0:m1, :].rearrange("p i m j -> p m j i"),
+                raw[:].rearrange("p j (m i) -> p m j i", i=PACK),
+            )
+
+        def quantize_w1(a, b, parts):
+            step = PASS // parts
+            flat = w1_bf[a, b][:].rearrange("p i m j -> p (i m j)")
+            for c in range(0, PASS, step):
+                nc.vector.quantize_mx(
+                    out=w1_q[a, b][:, c : c + step].bitcast(E4M3),
+                    scales=w1_s[a, b][:, c : c + step],
+                    in_=flat[:, PACK * c : PACK * (c + step)],
+                )
+
+        def h_pass(acc, a, b, i, s0):
+            nc.tensor.matmul_mx(
+                out=acc[:],
+                lhsT=w1_q[a, b][:, P * i : P * (i + 1)].bitcast(E4M3),
+                lhsT_scale=w1_s[a, b][:, P * i : P * (i + 1)],
+                rhs=v_w[a][:, s0 : s0 + BANK].bitcast(E4M3),
+                rhs_scale=v_s[4 * a : P, s0 : s0 + BANK],
+                start=(a == 0),
+                stop=(a == 1),
+            )
+
+        h = [held("h%d" % t, [P, S], F32) for t in range(8)]
+        tops = held("tops", [P, 16], F32, tag="late")
+        neg_ss = held("neg_ss", [P, 8], F32)
+        bias_a = held("bias_a", [P, 8], F32)
+
+        def leave_banks(t, accs):
+            for k, acc in enumerate(accs):
+                nc.vector.tensor_scalar(
+                    out=h[t][:, BANK * k : BANK * (k + 1)], in0=acc[:], scalar1=1.0, scalar2=None,
+                    op0=ALU.mult, op1=ALU.max, accum_out=tops[:, 2 * t + k : 2 * t + k + 1],
+                )
+            nc.vector.tensor_scalar(
+                out=bias_a[:, t : t + 1], in0=tops[:, 2 * t : 2 * t + 1], scalar1=tops[:, 2 * t + 1 : 2 * t + 2],
+                scalar2=neg_ss[:, t : t + 1], op0=ALU.max, op1=ALU.mult,
+            )
+
+        def look(dst, t, picks, m0, m1, scale, bias):
+            nc.scalar.activation(
+                out=dst, in_=h[t][:].indirect(picks[:, m0 // PER_COL : m1 // PER_COL]), func=ACT.Sigmoid,
+                bias=bias[:, t : t + 1], scale=scale[:, t : t + 1],
+            )
+
+        z_q = [held("z_q%d" % b, [P, PICK], U32) for b in range(2)]
+        z_s = [held("z_s%d" % b, [P, PICK], U8) for b in range(2)]
+
+        def interleave(engine, dst, src):
+            cast(
+                engine,
+                dst.rearrange("p (c e) i -> p c i e", e=PACK),
+                src.rearrange("p i (c e) -> p c i e", e=PACK),
+            )
+
+        def sheet_tiles(b, m0, m1, tag=None):
+            both = held("ac%d_%d" % (b, m0), [P, 2 * PACK * (m1 - m0)], F32, tag=tag)
+            view = both[:].rearrange("p (k i m) -> p k i m", k=2, i=PACK)
+            return view[:, 0, :, :], view[:, 1, :, :]
+
+        def looks(b, i, m0, m1, ac, gate_first):
+            t = PACK * b + i
+            if gate_first:
+                look(ac[1][:, i, :], t, p2, m0, m1, row["slope"], row["thr"])
+            look(ac[0][:, i, :], t, p1, m0, m1, row["sharp"], bias_a)
+            if not gate_first:
+                look(ac[1][:, i, :], t, p2, m0, m1, row["slope"], row["thr"])
+
+        def sheet_rows(b, i, m0, m1, ac):
+            t = PACK * b + i
+            nc.vector.tensor_tensor(out=ac[0][:, i, :], in0=ac[0][:, i, :], in1=score_sb[b][:, i, m0:m1], op=ALU.mult)
+            nc.vector.scalar_tensor_tensor(
+                out=ac[1][:, i, :], in0=ac[1][:, i, :], scalar=row["lean"][:, t : t + 1], in1=ac[0][:, i, :],
+                op0=ALU.mult, op1=ALU.add,
+            )
+
+        def quantize_sheet(b, m0, m1, ac):
+            z_bf = held("z_bf%d_%d" % (b, m0), [P, m1 - m0, PACK], BF16)
+            interleave("vector", z_bf[:], ac[1])
+            nc.vector.quantize_mx(
+                out=z_q[b][:, m0:m1].bitcast(E4M3), scales=z_s[b][:, m0:m1],
+                in_=z_bf[:].rearrange("p m i -> p (m i)"),
+            )
+
+        w2_q = [held("w2_q%d" % b, [P, N], U32) for b in range(2)]
+        w2_s = [held("w2_s%d" % b, [P, N], U8) for b in range(2)]
+
+        def quantize_w2(engine, b):
+            w2_bf = held("w2_bf%d" % b, [P, N, PACK], BF16)
+            interleave(engine, w2_bf[:], w2_raw[b][:])
+            nc.vector.quantize_mx(
+                out=w2_q[b][:].bitcast(E4M3), scales=w2_s[b][:], in_=w2_bf[:].rearrange("p n i -> p (n i)")
+            )
+
+        def out_pass(acc, b, nt, m0):
+            n0 = P * nt
+            z_codes = z_q[b][:, m0 : m0 + HALF].bitcast(E4M3)
+            z_plane = z_s[b][:, m0 : m0 + HALF]
+            nc.tensor.matmul_mx(
+                out=acc[:, HALF:BANK], lhsT=w2_q[b][:, n0 : n0 + P].bitcast(E4M3), lhsT_scale=w2_s[b][:, n0 : n0 + P],
+                rhs=z_codes, rhs_scale=z_plane, start=(b == 0), stop=False,
+            )
+            nc.tensor.matmul_mx(
+                out=acc[:, 0:HALF], lhsT=w4_w[:, b, 2 * n0 : 2 * (n0 + P)].bitcast(E2M1), lhsT_scale=w4_s[:, b, n0 : n0 + P],
+                rhs=z_codes, rhs_scale=z_plane, start=False, stop=(b == 1),
+            )
+
+        gather_words(0)
+        nc.vector.tensor_copy(out=v_s[:], in_=tab_s[:].indirect(idx[:]))
+        round_w1("scalar", 0, 0)
+        quantize_w1(0, 0, 1)
+        accs = {(i, k): psum.tile([P, BANK], F32, name="acc") for i in range(PACK) for k in range(2)}
+        for i in range(PACK):
+            for k in range(2):
+                h_pass(accs[i, k], 0, 0, i, BANK * k)
+        gather_words(1)
+        round_w1("scalar", 1, 0)
+        round_w1("vector", 1, 256)
+        quantize_w1(1, 0, 4)
+        round_w1("scalar", 0, 512)
+        ac0 = sheet_tiles(0, 0, PICK)
+        nc.vector.scalar_tensor_tensor(
+            out=neg_ss[:], in0=row["sharp"][:], scalar=-1.0, in1=row["share"][:], op0=ALU.mult, op1=ALU.mult
+        )
+        for i in range(PACK):
+            for k in range(2):
+                h_pass(accs[i, k], 1, 0, i, BANK * k)
+            leave_banks(i, [accs[i, 0], accs[i, 1]])
+            looks(0, i, 0, PICK, ac0, True)
+        round_w1("vector", 0, 768)
+        quantize_w1(0, 1, 1)
+        round_w1("vector", 1, 512)
+        quantize_w1(1, 1, 1)
+
+        for i in range(PACK):
+            pair = [psum.tile([P, BANK], F32, name="acc") for k in range(2)]
+            for k in range(2):
+                for a in range(2):
+                    h_pass(pair[k], a, 1, i, BANK * k)
+            leave_banks(PACK + i, pair)
+        for i in range(PACK):
+            sheet_rows(0, i, 0, PICK, ac0)
+        quantize_w2("scalar", 0)
+        quantize_sheet(0, 0, PICK, ac0)
+        quantize_w2("scalar", 1)
+
+        sums = {(m0, nt): psum.tile([P, BANK], F32, name="acc") for m0 in (0, HALF) for nt in range(N // P)}
+        for m0 in (0, HALF):
+            for nt in range(N // P):
+                out_pass(sums[m0, nt], 0, nt, m0)
+
+        halves = {}
+        for m0 in (0, HALF):
+            halves[m0] = sheet_tiles(1, m0, m0 + HALF, "late" if m0 else None)
+            for i in range(PACK):
+                looks(1, i, m0, m0 + HALF, halves[m0], False)
+        out_rows = out.rearrange("(nt p) m -> p nt m", p=P)
+        for m0 in (0, HALF):
+            for i in range(PACK):
+                sheet_rows(1, i, m0, m0 + HALF, halves[m0])
+            quantize_sheet(1, m0, m0 + HALF, halves[m0])
+            for nt in range(N // P):
+                out_pass(sums[m0, nt], 1, nt, m0)
+        for m0 in (0, HALF):
+            size = held("size%d" % m0, [P, N // P, HALF], F32)
+            res = held("res%d" % m0, [P, N // P, HALF], F32)
+            for nt in range(N // P):
+                acc = sums[m0, nt]
+                nc.scalar.activation(out=size[:, nt, :], in_=acc[:, HALF:BANK], func=ACT.Abs)
+                nc.vector.tensor_tensor(out=res[:, nt, :], in0=acc[:, 0:HALF], in1=size[:, nt, :], op=ALU.add)
+                if nt % 2 == 1:
+                    nc.sync.dma_start(
+                        out=out_rows[:, nt - 1 : nt + 1, m0 : m0 + HALF], in_=res[:, nt - 1 : nt + 1, :]
+                    )

@@ -2,8 +2,8 @@ from contextlib import ExitStack
 
 import concourse.mybir as mybir
 
-K, H, N, T, S, PICK = 1024, 1024, 512, 2048, 1024, 512
-FLOPS = 2 * K * H * S + 2 * 2 * H * N * PICK
+K, H, N, T, S, PICKS = 1024, 1024, 512, 2048, 1024, 512
+FLOPS = 2 * K * H * S + 2 * 2 * H * N * PICKS
 
 F32 = mybir.dt.float32
 BF16 = mybir.dt.bfloat16
@@ -20,8 +20,11 @@ P = 128
 PACK = 4
 PASS = P * PACK
 BANK = 512
-HALF = 256
-PER_COL = 16
+PER_COLUMN = 16
+HALF = PICKS // 2
+QUARTER = PICKS // 4
+W1_HALF = PASS // 2
+ROW_TILES = H // P
 
 
 def tile_list_band_adjudication_box_kernel(
@@ -33,233 +36,255 @@ def tile_list_band_adjudication_box_kernel(
         keep = ctx.enter_context(tc.tile_pool(name="keep", bufs=1))
         psum = ctx.enter_context(tc.psum_pool(name="psum", bufs=8))
 
-        def held(name, shape, dtype, tag=None):
-            return keep.tile(shape, dtype, name=name, tag=tag or name, align_bytes=64)
+        def held(name, shape, dtype, buffer=None):
+            return keep.tile(shape, dtype, name=name, tag=buffer or name, align_bytes=64)
 
-        def cast(engine, dst, src):
-            if engine == "scalar":
-                nc.scalar.copy(out=dst, in_=src)
-            else:
-                nc.vector.tensor_copy(out=dst, in_=src)
+        tab_plane = held("tab_plane", [P, T], U8)
+        nc.vector.memset(tab_plane[:].bitcast(I32), 0)
+        w4_plane = held("w4_plane", [P, 2, N], U8)
+        nc.gpsimd.memset(w4_plane[:].rearrange("p b n -> p (b n)").bitcast(I32), 0)
 
-        tab_s = held("tab_s", [P, T], U8)
-        nc.vector.memset(tab_s[:].bitcast(I32), 0)
-        w4_s = held("w4_s", [P, 2, N], U8)
-        nc.gpsimd.memset(w4_s[:].rearrange("p b n -> p (b n)").bitcast(I32), 0)
-
-        idx = held("idx", [P, S // PER_COL], U16)
-        p1 = held("p1", [P, PICK // PER_COL], U16)
-        p2 = held("p2", [P, PICK // PER_COL], U16)
-        tab_w = [held("tab_w%d" % a, [P, T], I32) for a in range(2)]
+        idx = held("idx", [P, S // PER_COLUMN], U16)
+        p1 = held("p1", [P, PICKS // PER_COLUMN], U16)
+        p2 = held("p2", [P, PICKS // PER_COLUMN], U16)
+        tab_sb = [held("tab_sb%d" % a, [P, T], I32) for a in range(2)]
         w1_raw = {}
-        row = {}
+        per_row = {}
 
-        def load_tab(a):
-            nc.sync.dma_start(out=tab_w[a][:], in_=tab_words[a].rearrange("p t i -> p (t i)").bitcast(I32))
+        def load_table(a):
+            nc.sync.dma_start(out=tab_sb[a][:], in_=tab_words[a].rearrange("p t i -> p (t i)").bitcast(I32))
 
         def load_w1(a, c0, c1):
             w1_raw[a, c0] = held("w1_raw%d_%d" % (a, c0), [P, PACK, c1 - c0], F32)
             rows = w1[PASS * a : PASS * (a + 1), c0:c1]
             nc.sync.dma_start(out=w1_raw[a, c0][:], in_=rows.rearrange("(p j) c -> p j c", j=PACK))
 
-        def load_rows(name, mat, b):
-            raw = held("%s%d" % (name, b), [P, PACK, mat.shape[1]], F32)
-            nc.sync.dma_start(out=raw[:], in_=mat[PASS * b : PASS * (b + 1), :].rearrange("(p i) c -> p i c", i=PACK))
+        def load_rows(name, matrix, b):
+            raw = held("%s%d" % (name, b), [P, PACK, matrix.shape[1]], F32)
+            rows = matrix[PASS * b : PASS * (b + 1), :]
+            nc.sync.dma_start(out=raw[:], in_=rows.rearrange("(p i) c -> p i c", i=PACK))
             return raw
 
-        def load_vector(name, vec):
-            row[name] = held(name, [P, 2 * PACK], F32)
+        def load_vector(name, vector):
+            per_row[name] = held(name, [P, ROW_TILES], F32)
             nc.sync.dma_start(
-                out=row[name][:].rearrange("p (b i) -> p b i", i=PACK),
-                in_=vec.rearrange("(b p i) -> p b i", p=P, i=PACK),
+                out=per_row[name][:].rearrange("p (b i) -> p b i", i=PACK),
+                in_=vector.rearrange("(b p i) -> p b i", p=P, i=PACK),
             )
 
         nc.sync.dma_start(idx[:], offs)
-        load_tab(0)
-        for q in range(4):
-            nc.scalar.dma_start(
-                out=tab_s[32 * q : 32 * q + 8, :].bitcast(I32), in_=tab_scales[:, 4 * q : 4 * q + 4, :].bitcast(I32)
-            )
-        load_w1(0, 0, 512)
-        load_tab(1)
-        load_w1(1, 0, 256)
-        load_w1(1, 256, 512)
-        load_w1(0, 512, 768)
         load_vector("slope", slope)
         load_vector("thr", thr)
-        nc.sync.dma_start(p2[:], pos2)
-        load_w1(0, 768, 1024)
+        load_table(0)
         load_vector("sharp", sharp)
-        load_vector("share", share)
-        nc.sync.dma_start(p1[:], pos1)
-        load_w1(1, 512, 1024)
-        load_vector("lean", lean)
-        score_sb = [load_rows("score", score, 0)]
-        w2_raw = [load_rows("w2_raw", w2, 0), load_rows("w2_raw", w2, 1)]
-        score_sb.append(load_rows("score", score, 1))
-        w4_w = held("w4_w", [P, 2, 2 * N], U8)
-        nc.sync.dma_start(out=w4_w[:].bitcast(I32), in_=w4_words.rearrange("b p e -> p b e").bitcast(I32))
         for q in range(4):
             nc.sync.dma_start(
-                out=w4_s[32 * q : 32 * q + 4, :, :].bitcast(I32),
+                out=tab_plane[32 * q : 32 * q + 8, :].bitcast(I32),
+                in_=tab_scales[:, 4 * q : 4 * q + 4, :].bitcast(I32),
+            )
+        load_vector("share", share)
+        load_w1(0, 0, W1_HALF)
+        load_w1(0, W1_HALF, PASS)
+        load_table(1)
+        load_w1(1, 0, W1_HALF)
+        load_w1(1, W1_HALF, PASS)
+        nc.sync.dma_start(p2[:], pos2)
+        load_w1(0, PASS, PASS + W1_HALF)
+        nc.sync.dma_start(p1[:], pos1)
+        load_w1(0, PASS + W1_HALF, H)
+        load_w1(1, PASS, H)
+        load_vector("lean", lean)
+        score_sb = [load_rows("score", score, 0)]
+        w2_raw = [load_rows("w2_raw", w2, b) for b in range(2)]
+        score_sb.append(load_rows("score", score, 1))
+        w4_codes = held("w4_codes", [P, 2, 2 * N], U8)
+        nc.sync.dma_start(out=w4_codes[:].bitcast(I32), in_=w4_words.rearrange("b p e -> p b e").bitcast(I32))
+        for q in range(4):
+            nc.sync.dma_start(
+                out=w4_plane[32 * q : 32 * q + 4, :, :].bitcast(I32),
                 in_=w4_scales[:, 4 * q : 4 * q + 4, :].rearrange("b r n -> r b n").bitcast(I32),
             )
 
-        v_w = [held("v_w%d" % a, [P, S], U32) for a in range(2)]
-        v_s = held("v_s", [P, S], U8)
+        v_codes = {}
+        v_plane = held("v_plane", [P, S], U8)
+        w1_bf = {}
+        blocks = [(a, b) for a in range(2) for b in range(2)]
+        w1_codes = {(a, b): held("w1_codes%d%d" % (a, b), [P, PASS], U32) for a, b in blocks}
+        w1_plane = {(a, b): held("w1_plane%d%d" % (a, b), [P, PASS], U8) for a, b in blocks}
+        h = [held("h%d" % t, [P, S], F32) for t in range(ROW_TILES)]
+        tops = held("tops", [P, 2 * ROW_TILES], F32, "after_h")
+        neg_gain = held("neg_gain", [P, ROW_TILES], F32)
+        bias_a = held("bias_a", [P, ROW_TILES], F32)
 
-        def gather_words(a):
+        def gather_words(a, buffer=None):
+            v_codes[a] = held("v_codes%d" % a, [P, S], U32, buffer)
             for s0 in range(0, S, BANK):
                 nc.vector.tensor_copy(
-                    out=v_w[a][:, s0 : s0 + BANK],
-                    in_=tab_w[a][:].bitcast(U32).indirect(idx[:, s0 // PER_COL : (s0 + BANK) // PER_COL]),
+                    out=v_codes[a][:, s0 : s0 + BANK],
+                    in_=tab_sb[a][:].bitcast(U32).indirect(idx[:, s0 // PER_COLUMN : (s0 + BANK) // PER_COLUMN]),
                 )
 
-        w1_bf = {(a, b): held("w1_bf%d%d" % (a, b), [P, PACK, P, PACK], BF16) for a in range(2) for b in range(2)}
-        w1_q = {(a, b): held("w1_q%d%d" % (a, b), [P, PASS], U32) for a in range(2) for b in range(2)}
-        w1_s = {(a, b): held("w1_s%d%d" % (a, b), [P, PASS], U8) for a in range(2) for b in range(2)}
-
-        def round_w1(engine, a, c0):
+        def round_w1(copy, a, c0):
             raw = w1_raw[a, c0]
             b, m0 = c0 // PASS, (c0 % PASS) // PACK
-            m1 = m0 + raw.shape[2] // PACK
-            cast(
-                engine,
-                w1_bf[a, b][:, :, m0:m1, :].rearrange("p i m j -> p m j i"),
-                raw[:].rearrange("p j (m i) -> p m j i", i=PACK),
+            copy(
+                out=w1_bf[a, b][:, :, m0 : m0 + raw.shape[2] // PACK, :].rearrange("p i m j -> p m j i"),
+                in_=raw[:].rearrange("p j (m i) -> p m j i", i=PACK),
             )
 
-        def quantize_w1(a, b, parts):
-            step = PASS // parts
+        def quantize_w1(a, b, width):
             flat = w1_bf[a, b][:].rearrange("p i m j -> p (i m j)")
-            for c in range(0, PASS, step):
+            for c in range(0, PASS, width):
                 nc.vector.quantize_mx(
-                    out=w1_q[a, b][:, c : c + step].bitcast(E4M3),
-                    scales=w1_s[a, b][:, c : c + step],
-                    in_=flat[:, PACK * c : PACK * (c + step)],
+                    out=w1_codes[a, b][:, c : c + width].bitcast(E4M3),
+                    scales=w1_plane[a, b][:, c : c + width],
+                    in_=flat[:, PACK * c : PACK * (c + width)],
                 )
 
         def h_pass(acc, a, b, i, s0):
             nc.tensor.matmul_mx(
                 out=acc[:],
-                lhsT=w1_q[a, b][:, P * i : P * (i + 1)].bitcast(E4M3),
-                lhsT_scale=w1_s[a, b][:, P * i : P * (i + 1)],
-                rhs=v_w[a][:, s0 : s0 + BANK].bitcast(E4M3),
-                rhs_scale=v_s[4 * a : P, s0 : s0 + BANK],
+                lhsT=w1_codes[a, b][:, P * i : P * (i + 1)].bitcast(E4M3),
+                lhsT_scale=w1_plane[a, b][:, P * i : P * (i + 1)],
+                rhs=v_codes[a][:, s0 : s0 + BANK].bitcast(E4M3),
+                rhs_scale=v_plane[4 * a : P, s0 : s0 + BANK],
                 start=(a == 0),
                 stop=(a == 1),
             )
 
-        h = [held("h%d" % t, [P, S], F32) for t in range(8)]
-        tops = held("tops", [P, 16], F32, tag="late")
-        neg_ss = held("neg_ss", [P, 8], F32)
-        bias_a = held("bias_a", [P, 8], F32)
-
-        def leave_banks(t, accs):
-            for k, acc in enumerate(accs):
+        def leave_banks(t, pair):
+            for k, acc in enumerate(pair):
                 nc.vector.tensor_scalar(
                     out=h[t][:, BANK * k : BANK * (k + 1)], in0=acc[:], scalar1=1.0, scalar2=None,
                     op0=ALU.mult, op1=ALU.max, accum_out=tops[:, 2 * t + k : 2 * t + k + 1],
                 )
             nc.vector.tensor_scalar(
-                out=bias_a[:, t : t + 1], in0=tops[:, 2 * t : 2 * t + 1], scalar1=tops[:, 2 * t + 1 : 2 * t + 2],
-                scalar2=neg_ss[:, t : t + 1], op0=ALU.max, op1=ALU.mult,
+                out=tops[:, 2 * t : 2 * t + 1], in0=tops[:, 2 * t : 2 * t + 1], scalar1=tops[:, 2 * t + 1 : 2 * t + 2],
+                scalar2=neg_gain[:, t : t + 1], op0=ALU.max, op1=ALU.mult, accum_out=bias_a[:, t : t + 1],
             )
 
-        def look(dst, t, picks, m0, m1, scale, bias):
-            nc.scalar.activation(
-                out=dst, in_=h[t][:].indirect(picks[:, m0 // PER_COL : m1 // PER_COL]), func=ACT.Sigmoid,
-                bias=bias[:, t : t + 1], scale=scale[:, t : t + 1],
-            )
-
-        z_q = [held("z_q%d" % b, [P, PICK], U32) for b in range(2)]
-        z_s = [held("z_s%d" % b, [P, PICK], U8) for b in range(2)]
-
-        def interleave(engine, dst, src):
-            cast(
-                engine,
-                dst.rearrange("p (c e) i -> p c i e", e=PACK),
-                src.rearrange("p i (c e) -> p c i e", e=PACK),
-            )
-
-        def sheet_tiles(b, m0, m1, tag=None):
-            both = held("ac%d_%d" % (b, m0), [P, 2 * PACK * (m1 - m0)], F32, tag=tag)
+        def part_tiles(b, m0, m1, buffer=None):
+            both = held("ac%d_%d" % (b, m0), [P, 2 * PACK * (m1 - m0)], F32, buffer)
             view = both[:].rearrange("p (k i m) -> p k i m", k=2, i=PACK)
             return view[:, 0, :, :], view[:, 1, :, :]
 
-        def looks(b, i, m0, m1, ac, gate_first):
-            t = PACK * b + i
-            if gate_first:
-                look(ac[1][:, i, :], t, p2, m0, m1, row["slope"], row["thr"])
-            look(ac[0][:, i, :], t, p1, m0, m1, row["sharp"], bias_a)
-            if not gate_first:
-                look(ac[1][:, i, :], t, p2, m0, m1, row["slope"], row["thr"])
-
-        def sheet_rows(b, i, m0, m1, ac):
-            t = PACK * b + i
-            nc.vector.tensor_tensor(out=ac[0][:, i, :], in0=ac[0][:, i, :], in1=score_sb[b][:, i, m0:m1], op=ALU.mult)
-            nc.vector.scalar_tensor_tensor(
-                out=ac[1][:, i, :], in0=ac[1][:, i, :], scalar=row["lean"][:, t : t + 1], in1=ac[0][:, i, :],
-                op0=ALU.mult, op1=ALU.add,
+        def look(dst, t, picks, m0, m1, scale, bias):
+            nc.scalar.activation(
+                out=dst, in_=h[t][:].indirect(picks[:, m0 // PER_COLUMN : m1 // PER_COLUMN]), func=ACT.Sigmoid,
+                bias=bias[:, t : t + 1], scale=scale[:, t : t + 1],
             )
 
-        def quantize_sheet(b, m0, m1, ac):
-            z_bf = held("z_bf%d_%d" % (b, m0), [P, m1 - m0, PACK], BF16)
-            interleave("vector", z_bf[:], ac[1])
+        def look_a(b, i, m0, m1, part):
+            look(part[0][:, i, :], PACK * b + i, p1, m0, m1, per_row["sharp"], bias_a)
+
+        def look_c(b, i, m0, m1, part):
+            look(part[1][:, i, :], PACK * b + i, p2, m0, m1, per_row["slope"], per_row["thr"])
+
+        def sheet_rows(b, i, m0, m1, part):
+            a_rows, c_rows = part[0][:, i, :], part[1][:, i, :]
+            t = PACK * b + i
+            nc.vector.tensor_tensor(out=a_rows, in0=a_rows, in1=score_sb[b][:, i, m0:m1], op=ALU.mult)
+            nc.vector.scalar_tensor_tensor(
+                out=c_rows, in0=c_rows, scalar=per_row["lean"][:, t : t + 1], in1=a_rows, op0=ALU.mult, op1=ALU.add
+            )
+
+        def round_rows(copy, dst, src):
+            copy(
+                out=dst.rearrange("p (c e) i -> p c i e", e=PACK),
+                in_=src.rearrange("p i (c e) -> p c i e", e=PACK),
+            )
+
+        z_codes = [held("z_codes%d" % b, [P, PICKS], U32) for b in range(2)]
+        z_plane = [held("z_plane%d" % b, [P, PICKS], U8) for b in range(2)]
+        w2_codes = [held("w2_codes%d" % b, [P, N], U32) for b in range(2)]
+        w2_plane = [held("w2_plane%d" % b, [P, N], U8) for b in range(2)]
+
+        def quantize_sheet(b, m0, m1, z, buffer=None):
+            z_bf = held("z_bf%d_%d" % (b, m0), [P, m1 - m0, PACK], BF16, buffer)
+            round_rows(nc.vector.tensor_copy, z_bf[:], z)
             nc.vector.quantize_mx(
-                out=z_q[b][:, m0:m1].bitcast(E4M3), scales=z_s[b][:, m0:m1],
+                out=z_codes[b][:, m0:m1].bitcast(E4M3), scales=z_plane[b][:, m0:m1],
                 in_=z_bf[:].rearrange("p m i -> p (m i)"),
             )
 
-        w2_q = [held("w2_q%d" % b, [P, N], U32) for b in range(2)]
-        w2_s = [held("w2_s%d" % b, [P, N], U8) for b in range(2)]
-
-        def quantize_w2(engine, b):
+        def quantize_w2(copy, b):
             w2_bf = held("w2_bf%d" % b, [P, N, PACK], BF16)
-            interleave(engine, w2_bf[:], w2_raw[b][:])
+            round_rows(copy, w2_bf[:], w2_raw[b][:])
             nc.vector.quantize_mx(
-                out=w2_q[b][:].bitcast(E4M3), scales=w2_s[b][:], in_=w2_bf[:].rearrange("p n i -> p (n i)")
+                out=w2_codes[b][:].bitcast(E4M3), scales=w2_plane[b][:], in_=w2_bf[:].rearrange("p n i -> p (n i)")
             )
 
-        def out_pass(acc, b, nt, m0):
-            n0 = P * nt
-            z_codes = z_q[b][:, m0 : m0 + HALF].bitcast(E4M3)
-            z_plane = z_s[b][:, m0 : m0 + HALF]
-            nc.tensor.matmul_mx(
-                out=acc[:, HALF:BANK], lhsT=w2_q[b][:, n0 : n0 + P].bitcast(E4M3), lhsT_scale=w2_s[b][:, n0 : n0 + P],
-                rhs=z_codes, rhs_scale=z_plane, start=(b == 0), stop=False,
-            )
-            nc.tensor.matmul_mx(
-                out=acc[:, 0:HALF], lhsT=w4_w[:, b, 2 * n0 : 2 * (n0 + P)].bitcast(E2M1), lhsT_scale=w4_s[:, b, n0 : n0 + P],
-                rhs=z_codes, rhs_scale=z_plane, start=False, stop=(b == 1),
-            )
+        def out_banks(m0, m1):
+            tiles_a_bank = BANK // (2 * (m1 - m0))
+            return [
+                (psum.tile([P, BANK], F32, name="acc"), range(nt0, nt0 + tiles_a_bank))
+                for nt0 in range(0, N // P, tiles_a_bank)
+            ]
 
+        def out_pass(banks, b, m0, m1):
+            width = m1 - m0
+            codes = z_codes[b][:, m0:m1].bitcast(E4M3)
+            plane = z_plane[b][:, m0:m1]
+            for acc, tiles in banks:
+                for g, nt in enumerate(tiles):
+                    n0, c0 = P * nt, 2 * width * g
+                    nc.tensor.matmul_mx(
+                        out=acc[:, c0 + width : c0 + 2 * width],
+                        lhsT=w2_codes[b][:, n0 : n0 + P].bitcast(E4M3), lhsT_scale=w2_plane[b][:, n0 : n0 + P],
+                        rhs=codes, rhs_scale=plane, start=(b == 0 and g == 0), stop=False,
+                    )
+                    nc.tensor.matmul_mx(
+                        out=acc[:, c0 : c0 + width],
+                        lhsT=w4_codes[:, b, 2 * n0 : 2 * (n0 + P)].bitcast(E2M1),
+                        lhsT_scale=w4_plane[:, b, n0 : n0 + P],
+                        rhs=codes, rhs_scale=plane, start=False, stop=(b == 1 and g == len(tiles) - 1),
+                    )
+
+        def finish(banks, m0, m1):
+            size = held("size%d" % m0, [P, N // P, m1 - m0], F32)
+            result = held("result%d" % m0, [P, N // P, m1 - m0], F32)
+            out_rows = out.rearrange("(nt p) m -> p nt m", p=P)
+            for acc, tiles in banks:
+                sums = acc[:].rearrange("p (g k m) -> p g k m", k=2, m=m1 - m0)
+                own = slice(tiles.start, tiles.stop)
+                nc.scalar.activation(out=size[:, own, :], in_=sums[:, :, 1, :], func=ACT.Abs)
+                nc.vector.tensor_tensor(out=result[:, own, :], in0=sums[:, :, 0, :], in1=size[:, own, :], op=ALU.add)
+                if tiles.stop % 2 == 0:
+                    two = slice(tiles.stop - 2, tiles.stop)
+                    nc.sync.dma_start(out=out_rows[:, two, m0:m1], in_=result[:, two, :])
+
+        for a, b in blocks:
+            w1_bf[a, b] = held("w1_bf%d%d" % (a, b), [P, PACK, P, PACK], BF16)
         gather_words(0)
-        nc.vector.tensor_copy(out=v_s[:], in_=tab_s[:].indirect(idx[:]))
-        round_w1("scalar", 0, 0)
-        quantize_w1(0, 0, 1)
-        accs = {(i, k): psum.tile([P, BANK], F32, name="acc") for i in range(PACK) for k in range(2)}
+        nc.vector.tensor_copy(out=v_plane[:], in_=tab_plane[:].indirect(idx[:]))
+        round_w1(nc.scalar.copy, 0, 0)
+        round_w1(nc.scalar.copy, 0, W1_HALF)
+        quantize_w1(0, 0, PASS)
+        first = [[psum.tile([P, BANK], F32, name="acc") for k in range(2)] for i in range(PACK)]
         for i in range(PACK):
             for k in range(2):
-                h_pass(accs[i, k], 0, 0, i, BANK * k)
-        gather_words(1)
-        round_w1("scalar", 1, 0)
-        round_w1("vector", 1, 256)
-        quantize_w1(1, 0, 4)
-        round_w1("scalar", 0, 512)
-        ac0 = sheet_tiles(0, 0, PICK)
+                h_pass(first[i][k], 0, 0, i, BANK * k)
+        gather_words(1, "w1_bf00")
+        round_w1(nc.scalar.copy, 1, 0)
+        round_w1(nc.scalar.copy, 1, W1_HALF)
+        quantize_w1(1, 0, P)
+        round_w1(nc.scalar.copy, 0, PASS)
+        round_w1(nc.scalar.copy, 0, PASS + W1_HALF)
         nc.vector.scalar_tensor_tensor(
-            out=neg_ss[:], in0=row["sharp"][:], scalar=-1.0, in1=row["share"][:], op0=ALU.mult, op1=ALU.mult
+            out=neg_gain[:], in0=per_row["sharp"][:], scalar=-1.0, in1=per_row["share"][:], op0=ALU.mult, op1=ALU.mult
         )
+        part0 = part_tiles(0, 0, PICKS)
         for i in range(PACK):
             for k in range(2):
-                h_pass(accs[i, k], 1, 0, i, BANK * k)
-            leave_banks(i, [accs[i, 0], accs[i, 1]])
-            looks(0, i, 0, PICK, ac0, True)
-        round_w1("vector", 0, 768)
-        quantize_w1(0, 1, 1)
-        round_w1("vector", 1, 512)
-        quantize_w1(1, 1, 1)
+                h_pass(first[i][k], 1, 0, i, BANK * k)
+            leave_banks(i, first[i])
+            look_c(0, i, 0, PICKS, part0)
+            look_a(0, i, 0, PICKS, part0)
+            if i == 0:
+                quantize_w1(0, 1, PASS)
+            if i == PACK - 2:
+                round_w1(nc.vector.tensor_copy, 1, PASS)
+                quantize_w1(1, 1, PASS)
 
         for i in range(PACK):
             pair = [psum.tile([P, BANK], F32, name="acc") for k in range(2)]
@@ -267,37 +292,37 @@ def tile_list_band_adjudication_box_kernel(
                 for a in range(2):
                     h_pass(pair[k], a, 1, i, BANK * k)
             leave_banks(PACK + i, pair)
+
         for i in range(PACK):
-            sheet_rows(0, i, 0, PICK, ac0)
-        quantize_w2("scalar", 0)
-        quantize_sheet(0, 0, PICK, ac0)
-        quantize_w2("scalar", 1)
+            sheet_rows(0, i, 0, PICKS, part0)
+        quantize_w2(nc.scalar.copy, 0)
+        quantize_sheet(0, 0, HALF, part0[1][:, :, 0:HALF])
+        quantize_w2(nc.vector.tensor_copy, 1)
+        half_banks = out_banks(0, HALF)
+        out_pass(half_banks, 0, 0, HALF)
+        quarters = [(m0, m0 + QUARTER) for m0 in (HALF, HALF + QUARTER)]
+        quarter_banks = [out_banks(m0, m1) for m0, m1 in quarters]
 
-        sums = {(m0, nt): psum.tile([P, BANK], F32, name="acc") for m0 in (0, HALF) for nt in range(N // P)}
-        for m0 in (0, HALF):
-            for nt in range(N // P):
-                out_pass(sums[m0, nt], 0, nt, m0)
+        part1 = part_tiles(1, 0, HALF)
+        part2 = part_tiles(1, HALF, PICKS, "after_h")
+        for part, m0 in ((part1, 0), (part2, HALF)):
+            for i in range(PACK):
+                look_a(1, i, m0, m0 + HALF, part)
+                look_c(1, i, m0, m0 + HALF, part)
 
-        halves = {}
-        for m0 in (0, HALF):
-            halves[m0] = sheet_tiles(1, m0, m0 + HALF, "late" if m0 else None)
-            for i in range(PACK):
-                looks(1, i, m0, m0 + HALF, halves[m0], False)
-        out_rows = out.rearrange("(nt p) m -> p nt m", p=P)
-        for m0 in (0, HALF):
-            for i in range(PACK):
-                sheet_rows(1, i, m0, m0 + HALF, halves[m0])
-            quantize_sheet(1, m0, m0 + HALF, halves[m0])
-            for nt in range(N // P):
-                out_pass(sums[m0, nt], 1, nt, m0)
-        for m0 in (0, HALF):
-            size = held("size%d" % m0, [P, N // P, HALF], F32)
-            res = held("res%d" % m0, [P, N // P, HALF], F32)
-            for nt in range(N // P):
-                acc = sums[m0, nt]
-                nc.scalar.activation(out=size[:, nt, :], in_=acc[:, HALF:BANK], func=ACT.Abs)
-                nc.vector.tensor_tensor(out=res[:, nt, :], in0=acc[:, 0:HALF], in1=size[:, nt, :], op=ALU.add)
-                if nt % 2 == 1:
-                    nc.sync.dma_start(
-                        out=out_rows[:, nt - 1 : nt + 1, m0 : m0 + HALF], in_=res[:, nt - 1 : nt + 1, :]
-                    )
+        for i in range(PACK):
+            sheet_rows(1, i, 0, HALF, part1)
+        quantize_sheet(1, 0, HALF, part1[1], "z_late")
+        out_pass(half_banks, 1, 0, HALF)
+        quantize_sheet(0, HALF, PICKS, part0[1][:, :, HALF:PICKS], "z_late")
+        for banks, (m0, m1) in zip(quarter_banks, quarters):
+            out_pass(banks, 0, m0, m1)
+        for i in range(PACK):
+            sheet_rows(1, i, HALF, PICKS, part2)
+        for banks, (m0, m1) in zip(quarter_banks, quarters):
+            quantize_sheet(1, m0, m1, part2[1][:, :, m0 - HALF : m1 - HALF])
+            out_pass(banks, 1, m0, m1)
+
+        finish(half_banks, 0, HALF)
+        for banks, (m0, m1) in zip(quarter_banks, quarters):
+            finish(banks, m0, m1)

@@ -19,6 +19,7 @@ ACT = mybir.ActivationFunctionType
 P = 128
 PACK = 4
 PASS = P * PACK
+GROUP = 32
 BANK = 512
 PER_COLUMN = 16
 HALF = PICKS // 2
@@ -42,14 +43,15 @@ def tile_list_band_adjudication_box_kernel(
         tab_plane = held("tab_plane", [P, T], U8)
         nc.vector.memset(tab_plane[:].bitcast(I32), 0)
         w4_plane = held("w4_plane", [P, 2, N], U8)
-        nc.gpsimd.memset(w4_plane[:].rearrange("p b n -> p (b n)").bitcast(I32), 0)
+        nc.vector.memset(w4_plane[:].rearrange("p b n -> p (b n)").bitcast(I32), 0)
+        dealt = held("dealt", [P, 2, PACK, GROUP], F32)
+        nc.vector.memset(dealt[:].rearrange("p b i x -> p (b i x)"), 0.0)
 
         idx = held("idx", [P, S // PER_COLUMN], U16)
         p1 = held("p1", [P, PICKS // PER_COLUMN], U16)
         p2 = held("p2", [P, PICKS // PER_COLUMN], U16)
         tab_sb = [held("tab_sb%d" % a, [P, T], I32) for a in range(2)]
         w1_raw = {}
-        per_row = {}
 
         def load_table(a):
             nc.sync.dma_start(out=tab_sb[a][:], in_=tab_words[a].rearrange("p t i -> p (t i)").bitcast(I32))
@@ -65,35 +67,29 @@ def tile_list_band_adjudication_box_kernel(
             nc.sync.dma_start(out=raw[:], in_=rows.rearrange("(p i) c -> p i c", i=PACK))
             return raw
 
-        def load_vector(name, vector):
-            per_row[name] = held(name, [P, ROW_TILES], F32)
+        vectors = (sharp, share, slope, thr, lean)
+        vector_runs = held("vector_runs", [P, 2, P], F32)
+        for v, vector in enumerate(vectors):
             nc.sync.dma_start(
-                out=per_row[name][:].rearrange("p (b i) -> p b i", i=PACK),
-                in_=vector.rearrange("(b p i) -> p b i", p=P, i=PACK),
+                out=vector_runs[v:P:GROUP, :, :], in_=vector.rearrange("(b g c) -> g b c", b=2, c=P)
             )
-
-        nc.sync.dma_start(idx[:], offs)
-        load_vector("slope", slope)
-        load_vector("thr", thr)
         load_table(0)
-        load_vector("sharp", sharp)
+        nc.sync.dma_start(idx[:], offs)
+        load_w1(0, 0, W1_HALF)
         for q in range(4):
             nc.sync.dma_start(
                 out=tab_plane[32 * q : 32 * q + 8, :].bitcast(I32),
                 in_=tab_scales[:, 4 * q : 4 * q + 4, :].bitcast(I32),
             )
-        load_vector("share", share)
-        load_w1(0, 0, W1_HALF)
         load_w1(0, W1_HALF, PASS)
         load_table(1)
         load_w1(1, 0, W1_HALF)
         load_w1(1, W1_HALF, PASS)
         nc.sync.dma_start(p2[:], pos2)
-        load_w1(0, PASS, PASS + W1_HALF)
         nc.sync.dma_start(p1[:], pos1)
+        load_w1(0, PASS, PASS + W1_HALF)
         load_w1(0, PASS + W1_HALF, H)
         load_w1(1, PASS, H)
-        load_vector("lean", lean)
         score_sb = [load_rows("score", score, 0)]
         w2_raw = [load_rows("w2_raw", w2, b) for b in range(2)]
         score_sb.append(load_rows("score", score, 1))
@@ -104,6 +100,17 @@ def tile_list_band_adjudication_box_kernel(
                 out=w4_plane[32 * q : 32 * q + 4, :, :].bitcast(I32),
                 in_=w4_scales[:, 4 * q : 4 * q + 4, :].rearrange("b r n -> r b n").bitcast(I32),
             )
+
+        per_row = held("per_row", [P, ROW_TILES, GROUP], F32)
+        for g0 in range(0, P, GROUP):
+            live = slice(g0, g0 + len(vectors))
+            nc.vector.tensor_copy(
+                out=dealt[live, :, :, :], in_=vector_runs[live, :, :].rearrange("p b (x i) -> p b i x", i=PACK)
+            )
+        nc.vector.transpose(
+            out=per_row[:].rearrange("p t v -> p (t v)"), in_=dealt[:].rearrange("p b i x -> p (b i x)")
+        )
+        sharp_sb, share_sb, slope_sb, thr_sb, lean_sb = [per_row[:, :, v] for v in range(len(vectors))]
 
         v_codes = {}
         v_plane = held("v_plane", [P, S], U8)
@@ -175,17 +182,18 @@ def tile_list_band_adjudication_box_kernel(
             )
 
         def look_a(b, i, m0, m1, part):
-            look(part[0][:, i, :], PACK * b + i, p1, m0, m1, per_row["sharp"], bias_a)
+            look(part[0][:, i, :], PACK * b + i, p1, m0, m1, sharp_sb, bias_a)
 
         def look_c(b, i, m0, m1, part):
-            look(part[1][:, i, :], PACK * b + i, p2, m0, m1, per_row["slope"], per_row["thr"])
+            look(part[1][:, i, :], PACK * b + i, p2, m0, m1, slope_sb, thr_sb)
 
-        def sheet_rows(b, i, m0, m1, part):
-            a_rows, c_rows = part[0][:, i, :], part[1][:, i, :]
+        def sheet_rows(engine, opened, b, i, m0, m1, part):
+            c_rows = part[1][:, i, :]
             t = PACK * b + i
-            nc.vector.tensor_tensor(out=a_rows, in0=a_rows, in1=score_sb[b][:, i, m0:m1], op=ALU.mult)
+            engine.tensor_tensor(out=opened[:, i, :], in0=part[0][:, i, :], in1=score_sb[b][:, i, m0:m1], op=ALU.mult)
             nc.vector.scalar_tensor_tensor(
-                out=c_rows, in0=c_rows, scalar=per_row["lean"][:, t : t + 1], in1=a_rows, op0=ALU.mult, op1=ALU.add
+                out=c_rows, in0=c_rows, scalar=lean_sb[:, t : t + 1], in1=opened[:, i, :],
+                op0=ALU.mult, op1=ALU.add,
             )
 
         def round_rows(copy, dst, src):
@@ -207,8 +215,8 @@ def tile_list_band_adjudication_box_kernel(
                 in_=z_bf[:].rearrange("p m i -> p (m i)"),
             )
 
-        def quantize_w2(copy, b):
-            w2_bf = held("w2_bf%d" % b, [P, N, PACK], BF16)
+        def quantize_w2(copy, b, buffer):
+            w2_bf = held("w2_bf%d" % b, [P, N, PACK], BF16, buffer)
             round_rows(copy, w2_bf[:], w2_raw[b][:])
             nc.vector.quantize_mx(
                 out=w2_codes[b][:].bitcast(E4M3), scales=w2_plane[b][:], in_=w2_bf[:].rearrange("p n i -> p (n i)")
@@ -266,12 +274,12 @@ def tile_list_band_adjudication_box_kernel(
                 h_pass(first[i][k], 0, 0, i, BANK * k)
         gather_words(1, "w1_bf00")
         round_w1(nc.scalar.copy, 1, 0)
-        round_w1(nc.scalar.copy, 1, W1_HALF)
+        round_w1(nc.vector.tensor_copy, 1, W1_HALF)
         quantize_w1(1, 0, P)
         round_w1(nc.scalar.copy, 0, PASS)
         round_w1(nc.scalar.copy, 0, PASS + W1_HALF)
         nc.vector.scalar_tensor_tensor(
-            out=neg_gain[:], in0=per_row["sharp"][:], scalar=-1.0, in1=per_row["share"][:], op0=ALU.mult, op1=ALU.mult
+            out=neg_gain[:], in0=sharp_sb, scalar=-1.0, in1=share_sb, op0=ALU.mult, op1=ALU.mult
         )
         part0 = part_tiles(0, 0, PICKS)
         for i in range(PACK):
@@ -293,11 +301,12 @@ def tile_list_band_adjudication_box_kernel(
                     h_pass(pair[k], a, 1, i, BANK * k)
             leave_banks(PACK + i, pair)
 
+        opened0 = held("opened0", [P, PACK, PICKS], F32, "w1_bf11")
         for i in range(PACK):
-            sheet_rows(0, i, 0, PICKS, part0)
-        quantize_w2(nc.scalar.copy, 0)
+            sheet_rows(nc.gpsimd if i < PACK - 1 else nc.vector, opened0, 0, i, 0, PICKS, part0)
+        quantize_w2(nc.scalar.copy, 0, "h3")
         quantize_sheet(0, 0, HALF, part0[1][:, :, 0:HALF])
-        quantize_w2(nc.vector.tensor_copy, 1)
+        quantize_w2(nc.vector.tensor_copy, 1, "neg_gain")
         half_banks = out_banks(0, HALF)
         out_pass(half_banks, 0, 0, HALF)
         quarters = [(m0, m0 + QUARTER) for m0 in (HALF, HALF + QUARTER)]
@@ -311,14 +320,14 @@ def tile_list_band_adjudication_box_kernel(
                 look_c(1, i, m0, m0 + HALF, part)
 
         for i in range(PACK):
-            sheet_rows(1, i, 0, HALF, part1)
+            sheet_rows(nc.vector, part1[0], 1, i, 0, HALF, part1)
         quantize_sheet(1, 0, HALF, part1[1], "z_late")
         out_pass(half_banks, 1, 0, HALF)
         quantize_sheet(0, HALF, PICKS, part0[1][:, :, HALF:PICKS], "z_late")
         for banks, (m0, m1) in zip(quarter_banks, quarters):
             out_pass(banks, 0, m0, m1)
         for i in range(PACK):
-            sheet_rows(1, i, HALF, PICKS, part2)
+            sheet_rows(nc.vector, part2[0], 1, i, HALF, PICKS, part2)
         for banks, (m0, m1) in zip(quarter_banks, quarters):
             quantize_sheet(1, m0, m1, part2[1][:, :, m0 - HALF : m1 - HALF])
             out_pass(banks, 1, m0, m1)

@@ -26,6 +26,7 @@ HALF = PICKS // 2
 QUARTER = PICKS // 4
 W1_HALF = PASS // 2
 ROW_TILES = H // P
+PLANE_ROWS = 4
 
 
 def tile_list_band_adjudication_box_kernel(
@@ -76,10 +77,10 @@ def tile_list_band_adjudication_box_kernel(
         load_table(0)
         nc.sync.dma_start(idx[:], offs)
         load_w1(0, 0, W1_HALF)
-        for q in range(4):
+        for g in range(P // GROUP):
             nc.sync.dma_start(
-                out=tab_plane[32 * q : 32 * q + 8, :].bitcast(I32),
-                in_=tab_scales[:, 4 * q : 4 * q + 4, :].bitcast(I32),
+                out=tab_plane[GROUP * g : GROUP * g + 2 * PLANE_ROWS, :].bitcast(I32),
+                in_=tab_scales[:, PLANE_ROWS * g : PLANE_ROWS * (g + 1), :].bitcast(I32),
             )
         load_w1(0, W1_HALF, PASS)
         load_table(1)
@@ -89,16 +90,17 @@ def tile_list_band_adjudication_box_kernel(
         nc.sync.dma_start(p1[:], pos1)
         load_w1(0, PASS, PASS + W1_HALF)
         load_w1(0, PASS + W1_HALF, H)
-        load_w1(1, PASS, H)
+        load_w1(1, PASS, PASS + W1_HALF)
+        load_w1(1, PASS + W1_HALF, H)
         score_sb = [load_rows("score", score, 0)]
         w2_raw = [load_rows("w2_raw", w2, b) for b in range(2)]
         score_sb.append(load_rows("score", score, 1))
         w4_codes = held("w4_codes", [P, 2, 2 * N], U8)
         nc.sync.dma_start(out=w4_codes[:].bitcast(I32), in_=w4_words.rearrange("b p e -> p b e").bitcast(I32))
-        for q in range(4):
+        for g in range(P // GROUP):
             nc.sync.dma_start(
-                out=w4_plane[32 * q : 32 * q + 4, :, :].bitcast(I32),
-                in_=w4_scales[:, 4 * q : 4 * q + 4, :].rearrange("b r n -> r b n").bitcast(I32),
+                out=w4_plane[GROUP * g : GROUP * g + PLANE_ROWS, :, :].bitcast(I32),
+                in_=w4_scales[:, PLANE_ROWS * g : PLANE_ROWS * (g + 1), :].rearrange("b r n -> r b n").bitcast(I32),
             )
 
         per_row = held("per_row", [P, ROW_TILES, GROUP], F32)
@@ -114,8 +116,8 @@ def tile_list_band_adjudication_box_kernel(
 
         v_codes = {}
         v_plane = held("v_plane", [P, S], U8)
-        w1_bf = {}
         blocks = [(a, b) for a in range(2) for b in range(2)]
+        w1_bf = {(a, b): held("w1_bf%d%d" % (a, b), [P, PACK, P, PACK], BF16) for a, b in blocks}
         w1_codes = {(a, b): held("w1_codes%d%d" % (a, b), [P, PASS], U32) for a, b in blocks}
         w1_plane = {(a, b): held("w1_plane%d%d" % (a, b), [P, PASS], U8) for a, b in blocks}
         h = [held("h%d" % t, [P, S], F32) for t in range(ROW_TILES)]
@@ -131,13 +133,19 @@ def tile_list_band_adjudication_box_kernel(
                     in_=tab_sb[a][:].bitcast(U32).indirect(idx[:, s0 // PER_COLUMN : (s0 + BANK) // PER_COLUMN]),
                 )
 
-        def round_w1(copy, a, c0):
-            raw = w1_raw[a, c0]
-            b, m0 = c0 // PASS, (c0 % PASS) // PACK
+        def round_w1(copy, run, a, c0, lo=0, hi=W1_HALF):
+            b, first_column = divmod(c0 + lo, PASS)
+            m0, m1 = first_column // PACK, (first_column + hi - lo) // PACK
             copy(
-                out=w1_bf[a, b][:, :, m0 : m0 + raw.shape[2] // PACK, :].rearrange("p i m j -> p m j i"),
-                in_=raw[:].rearrange("p j (m i) -> p m j i", i=PACK),
+                out=w1_bf[a, b][:, :, m0:m1, :].rearrange("p (u e) m j -> p m u j e", e=run),
+                in_=w1_raw[a, c0][:, :, lo:hi].rearrange("p j (m u e) -> p m u j e", u=PACK // run, e=run),
             )
+
+        def round_w1_scalar(*where):
+            round_w1(nc.scalar.copy, PACK, *where)
+
+        def round_w1_vector(*where):
+            round_w1(nc.vector.tensor_copy, PACK // 2, *where)
 
         def quantize_w1(a, b, width):
             flat = w1_bf[a, b][:].rearrange("p i m j -> p (i m j)")
@@ -154,7 +162,7 @@ def tile_list_band_adjudication_box_kernel(
                 lhsT=w1_codes[a, b][:, P * i : P * (i + 1)].bitcast(E4M3),
                 lhsT_scale=w1_plane[a, b][:, P * i : P * (i + 1)],
                 rhs=v_codes[a][:, s0 : s0 + BANK].bitcast(E4M3),
-                rhs_scale=v_plane[4 * a : P, s0 : s0 + BANK],
+                rhs_scale=v_plane[PLANE_ROWS * a : P, s0 : s0 + BANK],
                 start=(a == 0),
                 stop=(a == 1),
             )
@@ -261,23 +269,22 @@ def tile_list_band_adjudication_box_kernel(
                     two = slice(tiles.stop - 2, tiles.stop)
                     nc.sync.dma_start(out=out_rows[:, two, m0:m1], in_=result[:, two, :])
 
-        for a, b in blocks:
-            w1_bf[a, b] = held("w1_bf%d%d" % (a, b), [P, PACK, P, PACK], BF16)
         gather_words(0)
         nc.vector.tensor_copy(out=v_plane[:], in_=tab_plane[:].indirect(idx[:]))
-        round_w1(nc.scalar.copy, 0, 0)
-        round_w1(nc.scalar.copy, 0, W1_HALF)
+        round_w1_scalar(0, 0)
+        round_w1_scalar(0, W1_HALF)
         quantize_w1(0, 0, PASS)
         first = [[psum.tile([P, BANK], F32, name="acc") for k in range(2)] for i in range(PACK)]
         for i in range(PACK):
             for k in range(2):
                 h_pass(first[i][k], 0, 0, i, BANK * k)
         gather_words(1, "w1_bf00")
-        round_w1(nc.scalar.copy, 1, 0)
-        round_w1(nc.vector.tensor_copy, 1, W1_HALF)
+        round_w1_scalar(1, 0)
+        round_w1_scalar(1, W1_HALF, 0, W1_HALF // 2)
+        round_w1_vector(1, W1_HALF, W1_HALF // 2, W1_HALF)
         quantize_w1(1, 0, P)
-        round_w1(nc.scalar.copy, 0, PASS)
-        round_w1(nc.scalar.copy, 0, PASS + W1_HALF)
+        round_w1_scalar(0, PASS)
+        round_w1_scalar(0, PASS + W1_HALF)
         nc.vector.scalar_tensor_tensor(
             out=neg_gain[:], in0=sharp_sb, scalar=-1.0, in1=share_sb, op0=ALU.mult, op1=ALU.mult
         )
@@ -290,8 +297,9 @@ def tile_list_band_adjudication_box_kernel(
             look_a(0, i, 0, PICKS, part0)
             if i == 0:
                 quantize_w1(0, 1, PASS)
-            if i == PACK - 2:
-                round_w1(nc.vector.tensor_copy, 1, PASS)
+            if i == 1:
+                round_w1_vector(1, PASS)
+                round_w1_vector(1, PASS + W1_HALF)
                 quantize_w1(1, 1, PASS)
 
         for i in range(PACK):
@@ -303,7 +311,7 @@ def tile_list_band_adjudication_box_kernel(
 
         opened0 = held("opened0", [P, PACK, PICKS], F32, "w1_bf11")
         for i in range(PACK):
-            sheet_rows(nc.gpsimd if i < PACK - 1 else nc.vector, opened0, 0, i, 0, PICKS, part0)
+            sheet_rows(nc.gpsimd, opened0, 0, i, 0, PICKS, part0)
         quantize_w2(nc.scalar.copy, 0, "h3")
         quantize_sheet(0, 0, HALF, part0[1][:, :, 0:HALF])
         quantize_w2(nc.vector.tensor_copy, 1, "neg_gain")

from contextlib import ExitStack

import concourse.mybir as mybir

K, H, N, T, S, PICKS = 1024, 1024, 512, 2048, 1024, 512
FLOPS = 2 * K * H * S + 2 * 2 * H * N * PICKS

F32 = mybir.dt.float32
BF16 = mybir.dt.bfloat16
I32 = mybir.dt.int32
U32 = mybir.dt.uint32
U16 = mybir.dt.uint16
U8 = mybir.dt.uint8
E4M3 = mybir.dt.float8_e4m3fn_x4
E2M1 = mybir.dt.float4_e2m1fn_x4
ALU = mybir.AluOpType
ACT = mybir.ActivationFunctionType

P = 128
PACK = 4
PASS = P * PACK
GROUP = 32
BANK = 512
PER_COLUMN = 16
HALF = PICKS // 2
QUARTER = PICKS // 4
W1_HALF = PASS // 2
ROW_TILES = H // P
PLANE_ROWS = 4


def tile_list_band_adjudication_box_kernel(
    tc, tab_words, tab_scales, offs, pos1, pos2, w1, sharp, share, slope, thr, score, lean, w4_words, w4_scales, w2, out
):
    nc = tc.nc

    with ExitStack() as ctx:
        keep = ctx.enter_context(tc.tile_pool(name="keep", bufs=1))
        psum = ctx.enter_context(tc.psum_pool(name="psum", bufs=8))

        def held(name, shape, dtype, buffer=None):
            return keep.tile(shape, dtype, name=name, tag=buffer or name, align_bytes=64)

        tab_plane = held("tab_plane", [P, T], U8)
        nc.vector.memset(tab_plane[:].bitcast(I32), 0)
        w4_plane = held("w4_plane", [P, 2, N], U8)
        nc.vector.memset(w4_plane[:].rearrange("p b n -> p (b n)").bitcast(I32), 0)
        dealt = held("dealt", [P, 2, PACK, GROUP], F32)
        nc.vector.memset(dealt[:].rearrange("p b i x -> p (b i x)"), 0.0)

        idx = held("idx", [P, S // PER_COLUMN], U16)
        p1 = held("p1", [P, PICKS // PER_COLUMN], U16)
        p2 = held("p2", [P, PICKS // PER_COLUMN], U16)
        tab_sb = [held("tab_sb%d" % a, [P, T], I32) for a in range(2)]
        w1_raw = {}

        def load_table(a):
            nc.sync.dma_start(out=tab_sb[a][:], in_=tab_words[a].rearrange("p t i -> p (t i)").bitcast(I32))

        def load_w1(a, c0, c1):
            w1_raw[a, c0] = held("w1_raw%d_%d" % (a, c0), [P, PACK, c1 - c0], F32)
            rows = w1[PASS * a : PASS * (a + 1), c0:c1]
            nc.sync.dma_start(out=w1_raw[a, c0][:], in_=rows.rearrange("(p j) c -> p j c", j=PACK))

        def load_rows(name, matrix, b):
            raw = held("%s%d" % (name, b), [P, PACK, matrix.shape[1]], F32)
            rows = matrix[PASS * b : PASS * (b + 1), :]
            nc.sync.dma_start(out=raw[:], in_=rows.rearrange("(p i) c -> p i c", i=PACK))
            return raw

        vectors = (sharp, share, slope, thr, lean)
        vector_runs = held("vector_runs", [P, 2, P], F32)
        for v, vector in enumerate(vectors):
            nc.sync.dma_start(
                out=vector_runs[v:P:GROUP, :, :], in_=vector.rearrange("(b g c) -> g b c", b=2, c=P)
            )
        load_table(0)
        nc.sync.dma_start(idx[:], offs)
        load_w1(0, 0, W1_HALF)
        for g in range(P // GROUP):
            nc.sync.dma_start(
                out=tab_plane[GROUP * g : GROUP * g + 2 * PLANE_ROWS, :].bitcast(I32),
                in_=tab_scales[:, PLANE_ROWS * g : PLANE_ROWS * (g + 1), :].bitcast(I32),
            )
        load_w1(0, W1_HALF, PASS)
        load_table(1)
        load_w1(1, 0, W1_HALF)
        load_w1(1, W1_HALF, PASS)
        nc.sync.dma_start(p2[:], pos2)
        nc.sync.dma_start(p1[:], pos1)
        load_w1(0, PASS, PASS + W1_HALF)
        load_w1(0, PASS + W1_HALF, H)
        load_w1(1, PASS, PASS + W1_HALF)
        load_w1(1, PASS + W1_HALF, H)
        score_sb = [load_rows("score", score, 0)]
        w2_raw = [load_rows("w2_raw", w2, b) for b in range(2)]
        score_sb.append(load_rows("score", score, 1))
        w4_codes = held("w4_codes", [P, 2, 2 * N], U8)
        nc.sync.dma_start(out=w4_codes[:].bitcast(I32), in_=w4_words.rearrange("b p e -> p b e").bitcast(I32))
        for g in range(P // GROUP):
            nc.sync.dma_start(
                out=w4_plane[GROUP * g : GROUP * g + PLANE_ROWS, :, :].bitcast(I32),
                in_=w4_scales[:, PLANE_ROWS * g : PLANE_ROWS * (g + 1), :].rearrange("b r n -> r b n").bitcast(I32),
            )

        per_row = held("per_row", [P, ROW_TILES, GROUP], F32)
        for g0 in range(0, P, GROUP):
            live = slice(g0, g0 + len(vectors))
            nc.vector.tensor_copy(
                out=dealt[live, :, :, :], in_=vector_runs[live, :, :].rearrange("p b (x i) -> p b i x", i=PACK)
            )
        nc.vector.transpose(
            out=per_row[:].rearrange("p t v -> p (t v)"), in_=dealt[:].rearrange("p b i x -> p (b i x)")
        )
        sharp_sb, share_sb, slope_sb, thr_sb, lean_sb = [per_row[:, :, v] for v in range(len(vectors))]

        v_codes = {}
        v_plane = held("v_plane", [P, S], U8)
        blocks = [(a, b) for a in range(2) for b in range(2)]
        w1_bf = {(a, b): held("w1_bf%d%d" % (a, b), [P, PACK, P, PACK], BF16) for a, b in blocks}
        w1_codes = {(a, b): held("w1_codes%d%d" % (a, b), [P, PASS], U32) for a, b in blocks}
        w1_plane = {(a, b): held("w1_plane%d%d" % (a, b), [P, PASS], U8) for a, b in blocks}
        h = [held("h%d" % t, [P, S], F32) for t in range(ROW_TILES)]
        tops = held("tops", [P, 2 * ROW_TILES], F32, "after_h")
        neg_gain = held("neg_gain", [P, ROW_TILES], F32)
        bias_a = held("bias_a", [P, ROW_TILES], F32)

        def gather_words(a, buffer=None):
            v_codes[a] = held("v_codes%d" % a, [P, S], U32, buffer)
            for s0 in range(0, S, BANK):
                nc.vector.tensor_copy(
                    out=v_codes[a][:, s0 : s0 + BANK],
                    in_=tab_sb[a][:].bitcast(U32).indirect(idx[:, s0 // PER_COLUMN : (s0 + BANK) // PER_COLUMN]),
                )

        def round_w1(copy, run, a, c0, lo=0, hi=W1_HALF):
            b, first_column = divmod(c0 + lo, PASS)
            m0, m1 = first_column // PACK, (first_column + hi - lo) // PACK
            copy(
                out=w1_bf[a, b][:, :, m0:m1, :].rearrange("p (u e) m j -> p m u j e", e=run),
                in_=w1_raw[a, c0][:, :, lo:hi].rearrange("p j (m u e) -> p m u j e", u=PACK // run, e=run),
            )

        def round_w1_scalar(*where):
            round_w1(nc.scalar.copy, PACK, *where)

        def round_w1_vector(*where):
            round_w1(nc.vector.tensor_copy, PACK // 2, *where)

        def quantize_w1(a, b, width):
            flat = w1_bf[a, b][:].rearrange("p i m j -> p (i m j)")
            for c in range(0, PASS, width):
                nc.vector.quantize_mx(
                    out=w1_codes[a, b][:, c : c + width].bitcast(E4M3),
                    scales=w1_plane[a, b][:, c : c + width],
                    in_=flat[:, PACK * c : PACK * (c + width)],
                )

        def h_pass(acc, a, b, i, s0):
            nc.tensor.matmul_mx(
                out=acc[:],
                lhsT=w1_codes[a, b][:, P * i : P * (i + 1)].bitcast(E4M3),
                lhsT_scale=w1_plane[a, b][:, P * i : P * (i + 1)],
                rhs=v_codes[a][:, s0 : s0 + BANK].bitcast(E4M3),
                rhs_scale=v_plane[PLANE_ROWS * a : P, s0 : s0 + BANK],
                start=(a == 0),
                stop=(a == 1),
            )

        def leave_banks(t, pair):
            for k, acc in enumerate(pair):
                nc.vector.tensor_scalar(
                    out=h[t][:, BANK * k : BANK * (k + 1)], in0=acc[:], scalar1=1.0, scalar2=None,
                    op0=ALU.mult, op1=ALU.max, accum_out=tops[:, 2 * t + k : 2 * t + k + 1],
                )
            nc.vector.tensor_scalar(
                out=tops[:, 2 * t : 2 * t + 1], in0=tops[:, 2 * t : 2 * t + 1], scalar1=tops[:, 2 * t + 1 : 2 * t + 2],
                scalar2=neg_gain[:, t : t + 1], op0=ALU.max, op1=ALU.mult, accum_out=bias_a[:, t : t + 1],
            )

        def part_tiles(b, m0, m1, buffer=None):
            both = held("ac%d_%d" % (b, m0), [P, 2 * PACK * (m1 - m0)], F32, buffer)
            view = both[:].rearrange("p (k i m) -> p k i m", k=2, i=PACK)
            return view[:, 0, :, :], view[:, 1, :, :]

        def look(dst, t, picks, m0, m1, scale, bias):
            nc.scalar.activation(
                out=dst, in_=h[t][:].indirect(picks[:, m0 // PER_COLUMN : m1 // PER_COLUMN]), func=ACT.Sigmoid,
                bias=bias[:, t : t + 1], scale=scale[:, t : t + 1],
            )

        def look_a(b, i, m0, m1, part):
            look(part[0][:, i, :], PACK * b + i, p1, m0, m1, sharp_sb, bias_a)

        def look_c(b, i, m0, m1, part):
            look(part[1][:, i, :], PACK * b + i, p2, m0, m1, slope_sb, thr_sb)

        def sheet_rows(engine, opened, b, i, m0, m1, part):
            c_rows = part[1][:, i, :]
            t = PACK * b + i
            engine.tensor_tensor(out=opened[:, i, :], in0=part[0][:, i, :], in1=score_sb[b][:, i, m0:m1], op=ALU.mult)
            nc.vector.scalar_tensor_tensor(
                out=c_rows, in0=c_rows, scalar=lean_sb[:, t : t + 1], in1=opened[:, i, :],
                op0=ALU.mult, op1=ALU.add,
            )

        def round_rows(copy, dst, src):
            copy(
                out=dst.rearrange("p (c e) i -> p c i e", e=PACK),
                in_=src.rearrange("p i (c e) -> p c i e", e=PACK),
            )

        z_codes = [held("z_codes%d" % b, [P, PICKS], U32) for b in range(2)]
        z_plane = [held("z_plane%d" % b, [P, PICKS], U8) for b in range(2)]
        w2_codes = [held("w2_codes%d" % b, [P, N], U32) for b in range(2)]
        w2_plane = [held("w2_plane%d" % b, [P, N], U8) for b in range(2)]

        def quantize_sheet(b, m0, m1, z, buffer=None):
            z_bf = held("z_bf%d_%d" % (b, m0), [P, m1 - m0, PACK], BF16, buffer)
            round_rows(nc.vector.tensor_copy, z_bf[:], z)
            nc.vector.quantize_mx(
                out=z_codes[b][:, m0:m1].bitcast(E4M3), scales=z_plane[b][:, m0:m1],
                in_=z_bf[:].rearrange("p m i -> p (m i)"),
            )

        def quantize_w2(copy, b, buffer):
            w2_bf = held("w2_bf%d" % b, [P, N, PACK], BF16, buffer)
            round_rows(copy, w2_bf[:], w2_raw[b][:])
            nc.vector.quantize_mx(
                out=w2_codes[b][:].bitcast(E4M3), scales=w2_plane[b][:], in_=w2_bf[:].rearrange("p n i -> p (n i)")
            )

        def out_banks(m0, m1):
            tiles_a_bank = BANK // (2 * (m1 - m0))
            return [
                (psum.tile([P, BANK], F32, name="acc"), range(nt0, nt0 + tiles_a_bank))
                for nt0 in range(0, N // P, tiles_a_bank)
            ]

        def out_pass(banks, b, m0, m1):
            width = m1 - m0
            codes = z_codes[b][:, m0:m1].bitcast(E4M3)
            plane = z_plane[b][:, m0:m1]
            for acc, tiles in banks:
                for g, nt in enumerate(tiles):
                    n0, c0 = P * nt, 2 * width * g
                    nc.tensor.matmul_mx(
                        out=acc[:, c0 + width : c0 + 2 * width],
                        lhsT=w2_codes[b][:, n0 : n0 + P].bitcast(E4M3), lhsT_scale=w2_plane[b][:, n0 : n0 + P],
                        rhs=codes, rhs_scale=plane, start=(b == 0 and g == 0), stop=False,
                    )
                    nc.tensor.matmul_mx(
                        out=acc[:, c0 : c0 + width],
                        lhsT=w4_codes[:, b, 2 * n0 : 2 * (n0 + P)].bitcast(E2M1),
                        lhsT_scale=w4_plane[:, b, n0 : n0 + P],
                        rhs=codes, rhs_scale=plane, start=False, stop=(b == 1 and g == len(tiles) - 1),
                    )

        def finish(banks, m0, m1):
            size = held("size%d" % m0, [P, N // P, m1 - m0], F32)
            result = held("result%d" % m0, [P, N // P, m1 - m0], F32)
            out_rows = out.rearrange("(nt p) m -> p nt m", p=P)
            for acc, tiles in banks:
                sums = acc[:].rearrange("p (g k m) -> p g k m", k=2, m=m1 - m0)
                own = slice(tiles.start, tiles.stop)
                nc.scalar.activation(out=size[:, own, :], in_=sums[:, :, 1, :], func=ACT.Abs)
                nc.vector.tensor_tensor(out=result[:, own, :], in0=sums[:, :, 0, :], in1=size[:, own, :], op=ALU.add)
                if tiles.stop % 2 == 0:
                    two = slice(tiles.stop - 2, tiles.stop)
                    nc.sync.dma_start(out=out_rows[:, two, m0:m1], in_=result[:, two, :])

        gather_words(0)
        nc.vector.tensor_copy(out=v_plane[:], in_=tab_plane[:].indirect(idx[:]))
        round_w1_scalar(0, 0)
        round_w1_scalar(0, W1_HALF)
        quantize_w1(0, 0, PASS)
        first = [[psum.tile([P, BANK], F32, name="acc") for k in range(2)] for i in range(PACK)]
        for i in range(PACK):
            for k in range(2):
                h_pass(first[i][k], 0, 0, i, BANK * k)
        gather_words(1, "w1_bf00")
        round_w1_scalar(1, 0)
        round_w1_scalar(1, W1_HALF, 0, W1_HALF // 2)
        round_w1_vector(1, W1_HALF, W1_HALF // 2, W1_HALF)
        quantize_w1(1, 0, P)
        round_w1_scalar(0, PASS)
        round_w1_scalar(0, PASS + W1_HALF)
        nc.vector.scalar_tensor_tensor(
            out=neg_gain[:], in0=sharp_sb, scalar=-1.0, in1=share_sb, op0=ALU.mult, op1=ALU.mult
        )
        part0 = part_tiles(0, 0, PICKS)
        for i in range(PACK):
            for k in range(2):
                h_pass(first[i][k], 1, 0, i, BANK * k)
            leave_banks(i, first[i])
            look_c(0, i, 0, PICKS, part0)
            look_a(0, i, 0, PICKS, part0)
            if i == 0:
                quantize_w1(0, 1, PASS)
            if i == 1:
                round_w1_vector(1, PASS)
                round_w1_vector(1, PASS + W1_HALF)
                quantize_w1(1, 1, PASS)

        for i in range(PACK):
            pair = [psum.tile([P, BANK], F32, name="acc") for k in range(2)]
            for k in range(2):
                for a in range(2):
                    h_pass(pair[k], a, 1, i, BANK * k)
            leave_banks(PACK + i, pair)

        opened0 = held("opened0", [P, PACK, PICKS], F32, "w1_bf11")
        for i in range(PACK):
            sheet_rows(nc.gpsimd, opened0, 0, i, 0, PICKS, part0)
        quantize_w2(nc.scalar.copy, 0, "h3")
        quantize_sheet(0, 0, HALF, part0[1][:, :, 0:HALF])
        quantize_w2(nc.vector.tensor_copy, 1, "neg_gain")
        half_banks = out_banks(0, HALF)
        out_pass(half_banks, 0, 0, HALF)
        quarters = [(m0, m0 + QUARTER) for m0 in (HALF, HALF + QUARTER)]
        quarter_banks = [out_banks(m0, m1) for m0, m1 in quarters]

        part1 = part_tiles(1, 0, HALF)
        part2 = part_tiles(1, HALF, PICKS, "after_h")
        for part, m0 in ((part1, 0), (part2, HALF)):
            for i in range(PACK):
                look_a(1, i, m0, m0 + HALF, part)
                look_c(1, i, m0, m0 + HALF, part)

        for i in range(PACK):
            sheet_rows(nc.vector, part1[0], 1, i, 0, HALF, part1)
        quantize_sheet(1, 0, HALF, part1[1], "z_late")
        out_pass(half_banks, 1, 0, HALF)
        quantize_sheet(0, HALF, PICKS, part0[1][:, :, HALF:PICKS], "z_late")
        for banks, (m0, m1) in zip(quarter_banks, quarters):
            out_pass(banks, 0, m0, m1)
        for i in range(PACK):
            sheet_rows(nc.vector, part2[0], 1, i, HALF, PICKS, part2)
        for banks, (m0, m1) in zip(quarter_banks, quarters):
            quantize_sheet(1, m0, m1, part2[1][:, :, m0 - HALF : m1 - HALF])
            out_pass(banks, 1, m0, m1)

        finish(half_banks, 0, HALF)
        for banks, (m0, m1) in zip(quarter_banks, quarters):
            finish(banks, m0, m1)
